import numpy as np, ml_dtypes
CORES = [36,164,52,180,100,228,116,244]
N = 8
TK = 128
COEF = [[3,1,1,1,1,1,1,1],[1,3,1,1,1,1,1,1],[1,1,3,1,1,1,1,1],[1,1,1,3,1,1,1,1],[1,1,1,1,3,1,1,1],[1,1,1,1,1,3,1,1],[1,1,1,1,1,1,3,1],[1,1,1,1,1,1,1,3]]
def setup_inputs(rng):
    return {"x": rng.standard_normal((N, 128, TK), dtype=np.float32).astype(ml_dtypes.bfloat16), "a": (rng.standard_normal((N, 128, 128), dtype=np.float32) / 11).astype(ml_dtypes.bfloat16)}
def setup_inputs_big(rng):
    d = setup_inputs(rng)
    for k in ("x", "a"): d[k] = (d[k].astype(np.float32) * 1024.0).astype(d[k].dtype)
    return d
def setup_inputs_small(rng):
    d = setup_inputs(rng)
    for k in ("x", "a"): d[k] = (d[k].astype(np.float32) * (1 / 1024.0)).astype(d[k].dtype)
    return d
def setup_inputs_apart(rng):
    d = setup_inputs(rng)
    f = (10.0 ** rng.permutation(np.linspace(-1.5, 1.5, N))).astype(np.float32).reshape(N, 1, 1)
    for k in ("x", "a"): d[k] = (d[k].astype(np.float32) * f).astype(d[k].dtype)
    return d
def reference(x, a):
    X, A = x.astype(np.float64), a.astype(np.float64)
    y = np.stack([A[r].T @ sum(COEF[r][j] * X[j] for j in range(N)) for r in range(N)])
    return {"y": y.astype(ml_dtypes.bfloat16)}

from concourse.bass import DstId, RemoteDMATransfer

NR = 8
W = 128

SCRATCH = {
    "land": ("sbuf", [128, NR * W], "bfloat16"),
    "a_sb": ("sbuf", [128, W], "bfloat16"),
    "y_sb": ("sbuf", [128, W], "bfloat16"),
    "acc": ("psum", [128, W], "float32"),
}
SEMAPHORES = ["x_in", "a_in", "sent", "mm", "cp", "st"] + ["arr%d" % j for j in range(NR)]


def rank_program(g, core, T, topo):
    r = T.rank_of(core)
    if r is None:
        return
    coef = T.tables["COEF"]
    n = len(T.cores)

    def slot(j):
        return T.land[:, j * W:(j + 1) * W]

    g.sync.dma_start(slot(r), T.x[:]).then_inc(T.sem.x_in, 16)
    g.sync.dma_start(T.a_sb[:], T.a[:]).then_inc(T.sem.a_in, 16)

    dests = [(r + s) % n for s in range(1, n) if coef[(r + s) % n][r] != 0]
    mask = topo.mask(core, T.cores[dests[0]])
    for d in dests:
        mask &= topo.mask(core, T.cores[d])
    engines = bin(mask).count("1")
    ids = []
    for d in dests:
        rid, pid = topo.addr(T.cores[d], core)
        ids.append(DstId(rid=rid, pnc=pid))
    g.wait_ge(T.sem.x_in, 16)
    g.remote_dma_fused(
        [RemoteDMATransfer(dst_ids=ids, dma_engine_mask=mask, remote_sem=T.sem["arr%d" % r],
                           srcs=[slot(r)], dsts=[slot(r) for _ in dests], alu_op=0)],
        local_sem=T.sem.sent)

    order = [r] + [(r - s) % n for s in range(1, n)]
    terms = []
    for j in order:
        c = coef[r][j]
        assert c >= 0
        terms += [j] * c
    g.tensor.wait_ge(T.sem.a_in, 16)
    g.tensor.wait_ge(T.sem.x_in, 16)
    seen = {r}
    for k, j in enumerate(terms):
        if j not in seen:
            seen.add(j)
            g.tensor.wait_ge(T.sem["arr%d" % j], engines)
        mmi = g.tensor.matmul(T.acc[:], T.a_sb[:], slot(j), k == 0, k == len(terms) - 1)
    mmi.then_inc(T.sem.mm, 1)

    g.vector.wait_ge(T.sem.mm, 1)
    g.vector.tensor_copy(T.y_sb[:], T.acc[:]).then_inc(T.sem.cp, 1)
    g.sync.wait_ge(T.sem.cp, 1)
    g.sync.dma_start(T.y[:], T.y_sb[:]).then_inc(T.sem.st, 16)
    g.sync.wait_ge(T.sem.st, 16)
    g.wait_ge(T.sem.sent, engines)
